import numpy as np
import ml_dtypes


def mxq(x, axis, fmt="e4m3"):
    dtype, down = {"e4m3": (ml_dtypes.float8_e4m3fn, 7), "e5m2": (ml_dtypes.float8_e5m2, 14)}[fmt]
    v = np.moveaxis(np.asarray(x, np.float32).astype(ml_dtypes.bfloat16).astype(np.float64), axis, -1)
    blocks = v.reshape(v.shape[:-1] + (-1, 32))
    amax = np.abs(blocks).max(-1, keepdims=True)
    byte = np.maximum(np.where(amax > 0, np.frexp(amax)[1] - 1 + 127, 0) - down, 1)
    scale = np.exp2(byte - 127.0)
    codes = (blocks / scale).astype(np.float32).astype(dtype).astype(np.float64)
    return np.moveaxis((codes * scale).reshape(v.shape), -1, axis)


WIDE = False


def mx_kscale(k):
    if not WIDE:
        return np.ones(k)
    levels = np.array([30, -30])
    if k % 512:
        return np.exp2(np.random.permutation(np.resize(levels, k // 32))).repeat(32)
    a = np.empty((k // 512, 16))
    for p in range(k // 512):
        a[p, :8] = np.random.permutation(np.resize(levels, 8))
        for g in range(8):
            far = levels[np.abs(levels - a[p, g]) >= 10]
            a[p, g + 8] = far[np.random.randint(len(far))]
    return np.exp2(a.ravel()).repeat(32)


def f64(x):
    return np.asarray(x).astype(np.float64)


def striped(idx):
    return np.tile(np.asarray(idx).reshape(-1, 16).T, (8, 1)).astype(np.uint16)


def unstriped(offs):
    return offs[:16].T.reshape(-1).astype(np.int64)


K, J, N, T, V = 256, 1024, 256, 2048, 2048


def setup_inputs():
    n = np.random.standard_normal
    idx = np.random.permutation(T)[:J]
    idx2 = np.random.permutation(V)[:J]
    fj = mx_kscale(J)
    return {
        "xf": (n((K, T)) * np.random.uniform(0.4, 1.6, (1, T))).astype(np.float32),
        "ca": (np.random.uniform(0.5, 1.5, (J, 1)) * fj[:, None]).astype(np.float32),
        "gt": (n((N, V)) * np.exp(0.5 * n((1, V)))).astype(np.float32),
        "rb": (np.random.uniform(0.5, 1.5, (1, J)) / fj).astype(np.float32),
        "cp": (np.random.uniform(0.4, 1.2, (N, 1))).astype(np.float32),
        "bn": (np.random.uniform(-0.5, 0.5, (1, N))).astype(np.float32),
        "offs": striped(idx),
        "offs2": striped(idx2),
    }


def reference(xf, ca, gt, rb, cp, bn, offs, offs2):
    idx = unstriped(offs)
    idx2 = unstriped(offs2)
    xj = f64(xf)[:, idx].T
    uj = xj / (np.mean(np.abs(xj), axis=1, keepdims=True) + 0.1) * f64(ca)
    gs = np.minimum(f64(gt)[:, idx2], f64(cp)) * f64(rb)
    gj = gs.T
    ujq = mxq(uj, 0, "e4m3")
    gjq = mxq(gj, 0, "e5m2")
    w = ujq.T @ gjq
    ew = np.exp(0.02 * w + f64(bn))
    y = 256.0 * ew / np.sum(ew, axis=1, keepdims=True)
    return y

@@ -1,0 +1,208 @@
+from contextlib import ExitStack
+
+import concourse.mybir as mybir
+from concourse.masks import make_identity
+
+K, J, N, T = 256, 1024, 256, 2048
+FLOPS = 2 * K * J * N
+
+F32 = mybir.dt.float32
+BF16 = mybir.dt.bfloat16
+U32 = mybir.dt.uint32
+U16 = mybir.dt.uint16
+U8 = mybir.dt.uint8
+E4M3 = mybir.dt.float8_e4m3fn_x4
+E5M2 = mybir.dt.float8_e5m2_x4
+ALU = mybir.AluOpType
+ACT = mybir.ActivationFunctionType
+
+P = 128
+PACK = 4
+PASS = P * PACK
+PASSES = J // PASS
+HALVES = 2
+PER_COLUMN = 16
+
+
+def tile_list_moment_sized_bounded_shares_kernel(tc, xf, ca, gt, rb, cp, bn, offs, offs2, out):
+    nc = tc.nc
+    with ExitStack() as ctx:
+        keep = ctx.enter_context(tc.tile_pool(name="keep", bufs=1))
+        psum = ctx.enter_context(tc.psum_pool(name="psum", bufs=1))
+
+        x_list = keep.tile([P, J // PER_COLUMN], U16, name="x_list")
+        g_list = keep.tile([P, J // PER_COLUMN], U16, name="g_list")
+        x_rows = [keep.tile([P, T], F32, name="x_rows%d" % h) for h in range(HALVES)]
+        g_rows = [keep.tile([P, T], F32, name="g_rows%d" % h) for h in range(HALVES)]
+        ca_sb = keep.tile([P, PASSES, PACK], F32, name="ca_sb")
+        rb_sb = keep.tile([P, PASSES, PACK], F32, name="rb_sb")
+        cp_sb = keep.tile([P, HALVES], F32, name="cp_sb")
+        bn_sb = keep.tile([P, HALVES], F32, name="bn_sb")
+        g_by_parity = gt.rearrange("(p h) v -> h p v", h=HALVES)
+
+        nc.scalar.dma_start(bn_sb[:], bn.rearrange("o (p h) -> p (o h)", h=HALVES))
+        nc.sync.dma_start(x_list[:], offs)
+        nc.sync.dma_start(x_rows[0][:], xf[0:P, :])
+        nc.sync.dma_start(x_rows[1][:], xf[P : 2 * P, :])
+        nc.sync.dma_start(ca_sb[:], ca.rearrange("(a p t) o -> p a (t o)", p=P, t=PACK))
+        nc.sync.dma_start(g_list[:], offs2)
+        nc.sync.dma_start(g_rows[0][:], g_by_parity[0])
+        nc.sync.dma_start(rb_sb[:], rb.rearrange("o (a p t) -> p (o a) t", p=P, t=PACK))
+        nc.sync.dma_start(cp_sb[:], cp.rearrange("(p h) o -> p (h o)", h=HALVES))
+        nc.sync.dma_start(g_rows[1][:], g_by_parity[1])
+
+        ident = keep.tile([P, P], F32, name="ident")
+        make_identity(nc, ident[:])
+
+        bn_ps = psum.tile([P, HALVES, P], F32, name="bn_ps", tag="g0")
+        for h in range(HALVES):
+            nc.tensor.transpose(bn_ps[:, h, :], bn_sb[:, h : h + 1].to_broadcast([P, P]), ident[:])
+        bn_all = keep.tile([P, HALVES, P], F32, name="bn_all")
+        nc.scalar.activation(bn_all[:], bn_ps[:], ACT.Copy)
+        rb_ps = [psum.tile([P, PACK, P], F32, name="rb_ps%d" % a, tag="rb%d" % a) for a in range(PASSES)]
+        for a in range(PASSES):
+            for t in range(PACK):
+                nc.tensor.transpose(rb_ps[a][:, t, :], rb_sb[:, a, t : t + 1].to_broadcast([P, P]), ident[:])
+
+        def slots(offsets, a):
+            return offsets[:, a * PASS // PER_COLUMN : (a + 1) * PASS // PER_COLUMN]
+
+        def x_gather(h, a):
+            nc.vector.tensor_copy(x_picked[h][a][:].rearrange("k (t p) -> k p t", t=PACK), x_rows[h][:].indirect(slots(x_list, a)))
+
+        def g_gather(h, a):
+            nc.scalar.activation(g_picked[h][a][:], g_rows[h][:].indirect(slots(g_list, a)), ACT.Copy)
+
+        x_picked = [[keep.tile([P, PASS], F32, name="x_picked%d%d" % (h, a)) for a in range(PASSES)] for h in range(HALVES)]
+        g_picked = [[keep.tile([P, PASS], F32, name="g_picked%d%d" % (h, a)) for a in range(PASSES)] for h in range(HALVES)]
+        x_ps = [[psum.tile([P, PACK, P], F32, name="x_ps%d%d" % (h, a), tag="x%d%d" % (h, a)) for a in range(PASSES)] for h in range(HALVES)]
+        mean_part = [keep.tile([P, HALVES, PACK], F32, name="mean_part%d" % a) for a in range(PASSES)]
+        magnitude = keep.tile([P, HALVES, PASSES, PACK, P], BF16, name="magnitude")
+
+        def x_turn(h, a):
+            for t in range(PACK):
+                nc.tensor.transpose(x_ps[h][a][:, t, :], x_picked[h][a][:, t * P : (t + 1) * P], ident[:])
+
+        def x_size(h, a):
+            for t in range(PACK):
+                nc.scalar.activation(magnitude[:, h, a, t, :], x_ps[h][a][:, t, :], ACT.Abs, scale=1.0 / K, accum_out=mean_part[a][:, h, t : t + 1])
+
+
+        u_codes = [keep.tile([P, K], U32, name="u_codes%d" % a, align_bytes=64) for a in range(PASSES)]
+        u_scales = [keep.tile([P, K], U8, name="u_scales%d" % a, align_bytes=64) for a in range(PASSES)]
+        u_bf = [keep.tile([P, K, PACK], BF16, name="u_bf%d" % a, align_bytes=64) for a in range(PASSES)]
+        denom = [keep.tile([P, PACK], F32, name="denom%d" % a) for a in range(PASSES)]
+        inverse = [keep.tile([P, PACK], F32, name="inverse%d" % a) for a in range(PASSES)]
+        factor = [keep.tile([P, PACK], F32, name="factor%d" % a) for a in range(PASSES)]
+
+        def u_factor(a):
+            nc.vector.scalar_tensor_tensor(denom[a][:], mean_part[a][:, 1, :], 0.1, mean_part[a][:, 0, :], ALU.add, ALU.add)
+            nc.vector.reciprocal(inverse[a][:], denom[a][:])
+            nc.vector.tensor_tensor(factor[a][:], inverse[a][:], ca_sb[:, a, :], ALU.mult)
+
+        def u_scale(a, h):
+            nc.vector.tensor_tensor(
+                u_bf[a][:, h * P : (h + 1) * P, :],
+                x_ps[h][a][:].rearrange("p t k -> p k t"),
+                factor[a][:].unsqueeze(1).to_broadcast([P, P, PACK]),
+                ALU.mult,
+            )
+
+        def u_quantise(a):
+            nc.vector.quantize_mx(out=u_codes[a][:].bitcast(E4M3), scales=u_scales[a][:], in_=u_bf[a][:].rearrange("p k t -> p (k t)"))
+
+        g_bf = [[keep.tile([P, PASS], BF16, name="g_bf%d%d" % (h, a)) for a in range(PASSES)] for h in range(HALVES)]
+        g_grouped = [[keep.tile([P, P * PACK], BF16, name="g_grouped%d%d" % (h, a), align_bytes=64) for a in range(PASSES)] for h in range(HALVES)]
+        g_codes = [[keep.tile([P, P], U32, name="g_codes%d%d" % (h, a), align_bytes=64) for a in range(PASSES)] for h in range(HALVES)]
+        g_scales = [[keep.tile([P, P], U8, name="g_scales%d%d" % (h, a), align_bytes=64) for a in range(PASSES)] for h in range(HALVES)]
+
+        def g_weigh(h, a):
+            nc.vector.scalar_tensor_tensor(
+                g_bf[h][a][:].rearrange("n (p t) -> n p t", t=PACK),
+                g_picked[h][a][:].rearrange("n (p t) -> n p t", t=PACK),
+                cp_sb[:, h : h + 1],
+                rb_ps[a][:].rearrange("n t p -> n p t"),
+                ALU.min,
+                ALU.mult,
+            )
+
+        def g_turn(h, a):
+            words = g_bf[h][a][:].bitcast(F32)
+            g_ps = psum.tile([P, 2, P], F32, name="g_ps%d%d" % (h, a), tag="g%d" % a)
+            for u in range(2):
+                nc.tensor.transpose(g_ps[:, u, :], words[:, u : PASS // 2 : 2], ident[:])
+            nc.scalar.copy(g_grouped[h][a][:].bitcast(F32).rearrange("p (n u) -> p n u", u=2), g_ps[:].rearrange("p u n -> p n u"))
+
+        def g_quantise(h, a):
+            nc.vector.quantize_mx(out=g_codes[h][a][:].bitcast(E5M2), scales=g_scales[h][a][:], in_=g_grouped[h][a][:])
+
+        logit = keep.tile([P, HALVES, HALVES, P], F32, name="logit")
+        neg_logit = [keep.tile([P, HALVES, P], F32, name="neg_logit%d" % kh) for kh in range(HALVES)]
+        neg_max = [keep.tile([P, HALVES], F32, name="neg_max%d" % kh) for kh in range(HALVES)]
+
+        def moment(h):
+            w_ps = psum.tile([P, HALVES, P], F32, name="w_ps%d" % h, tag="x%d0" % h)
+            for a in range(PASSES):
+                for kh in range(HALVES):
+                    nc.tensor.matmul_mx(
+                        out=w_ps[:, kh, :],
+                        lhsT=u_codes[a][:, kh * P : (kh + 1) * P].bitcast(E4M3),
+                        lhsT_scale=u_scales[a][:, kh * P : (kh + 1) * P],
+                        rhs=g_codes[h][a][:].bitcast(E5M2),
+                        rhs_scale=g_scales[h][a][:],
+                        start=(a == 0 and kh == 0),
+                        stop=(a == PASSES - 1 and kh == HALVES - 1),
+                    )
+            for kh in range(HALVES):
+                nc.vector.scalar_tensor_tensor(logit[:, h, kh, :], w_ps[:, kh, :], 0.02, bn_all[:, h, :], ALU.mult, ALU.add)
+            for kh in range(HALVES):
+                nc.vector.tensor_scalar(
+                    neg_logit[kh][:, h, :], logit[:, h, kh, :], -1.0, neg_max[kh][:, 0:1] if h else None,
+                    ALU.mult, ALU.min, accum_out=neg_max[kh][:, h : h + 1],
+                )
+
+        for h in range(HALVES):
+            for a in range(PASSES):
+                x_gather(h, a)
+                x_turn(h, a)
+                if (h, a) == (1, 1):
+                    g_gather(0, 0)
+                x_size(h, a)
+        g_gather(0, 1)
+        g_gather(1, 0)
+        g_gather(1, 1)
+        u_factor(0)
+        u_scale(0, 0)
+        u_scale(0, 1)
+        u_factor(1)
+        u_quantise(0)
+        u_scale(1, 0)
+        u_scale(1, 1)
+        g_weigh(0, 0)
+        u_quantise(1)
+        g_weigh(0, 1)
+        g_weigh(1, 0)
+        g_turn(0, 0)
+        g_turn(0, 1)
+        g_turn(1, 0)
+        g_weigh(1, 1)
+        g_quantise(0, 0)
+        g_quantise(0, 1)
+        g_turn(1, 1)
+        moment(0)
+        g_quantise(1, 0)
+        g_quantise(1, 1)
+        moment(1)
+
+        for kh in range(HALVES):
+            shares = keep.tile([P, P, HALVES], F32, name="shares%d" % kh)
+            total = keep.tile([P, 1], F32, name="total%d" % kh)
+            inv_total = keep.tile([P, 1], F32, name="inv_total%d" % kh)
+            result = keep.tile([P, N], F32, name="result%d" % kh)
+            nc.scalar.activation(
+                shares[:], neg_logit[kh][:].rearrange("k h p -> k p h"), ACT.Exp,
+                bias=neg_max[kh][:, 1:2], scale=-1.0, accum_out=total[:],
+            )
+            nc.vector.reciprocal(inv_total[:], total[:])
+            nc.vector.tensor_scalar(result[:], shares[:].rearrange("k p h -> k (p h)"), inv_total[:], 256.0, ALU.mult, ALU.mult)
+            nc.sync.dma_start(out[kh * P : (kh + 1) * P, :], result[:])

@@ -34,20 +34,20 @@ def tile_list_moment_sized_bounded_shares_kernel(tc, xf, ca, gt, rb, cp, bn, off
         g_list = keep.tile([P, J // PER_COLUMN], U16, name="g_list")
         x_rows = [keep.tile([P, T], F32, name="x_rows%d" % h) for h in range(HALVES)]
         g_rows = [keep.tile([P, T], F32, name="g_rows%d" % h) for h in range(HALVES)]
-        ca_sb = keep.tile([P, PASSES, PACK], F32, name="ca_sb")
-        rb_sb = keep.tile([P, PASSES, PACK], F32, name="rb_sb")
+        ca_sb = keep.tile([P, PASSES, 2 * PACK], F32, name="ca_sb")
+        rb_sb = keep.tile([P, PASSES, 2 * PACK], F32, name="rb_sb")
         cp_sb = keep.tile([P, HALVES], F32, name="cp_sb")
         bn_sb = keep.tile([P, HALVES], F32, name="bn_sb")
         g_by_parity = gt.rearrange("(p h) v -> h p v", h=HALVES)
 
         nc.scalar.dma_start(bn_sb[:], bn.rearrange("o (p h) -> p (o h)", h=HALVES))
+        nc.scalar.dma_start(rb_sb[:, :, 0:PACK], rb.rearrange("o (a p t) -> p (o a) t", p=P, t=PACK))
         nc.sync.dma_start(x_list[:], offs)
         nc.sync.dma_start(x_rows[0][:], xf[0:P, :])
         nc.sync.dma_start(x_rows[1][:], xf[P : 2 * P, :])
-        nc.sync.dma_start(ca_sb[:], ca.rearrange("(a p t) o -> p a (t o)", p=P, t=PACK))
+        nc.sync.dma_start(ca_sb[:, :, 0:PACK], ca.rearrange("(a p t) o -> p a (t o)", p=P, t=PACK))
         nc.sync.dma_start(g_list[:], offs2)
         nc.sync.dma_start(g_rows[0][:], g_by_parity[0])
-        nc.sync.dma_start(rb_sb[:], rb.rearrange("o (a p t) -> p (o a) t", p=P, t=PACK))
         nc.sync.dma_start(cp_sb[:], cp.rearrange("(p h) o -> p (h o)", h=HALVES))
         nc.sync.dma_start(g_rows[1][:], g_by_parity[1])
 
@@ -67,11 +67,17 @@ def tile_list_moment_sized_bounded_shares_kernel(tc, xf, ca, gt, rb, cp, bn, off
         def slots(offsets, a):
             return offsets[:, a * PASS // PER_COLUMN : (a + 1) * PASS // PER_COLUMN]
 
-        def x_gather(h, a):
-            nc.vector.tensor_copy(x_picked[h][a][:].rearrange("k (t p) -> k p t", t=PACK), x_rows[h][:].indirect(slots(x_list, a)))
+        def gather(engine, picked, rows, offsets, a):
+            if engine == "vector":
+                nc.vector.tensor_copy(picked[:], rows[:].indirect(slots(offsets, a)))
+            else:
+                nc.scalar.activation(picked[:], rows[:].indirect(slots(offsets, a)), ACT.Copy)
 
-        def g_gather(h, a):
-            nc.scalar.activation(g_picked[h][a][:], g_rows[h][:].indirect(slots(g_list, a)), ACT.Copy)
+        def x_gather(engine, h, a):
+            gather(engine, x_picked[h][a], x_rows[h], x_list, a)
+
+        def g_gather(engine, h, a):
+            gather(engine, g_picked[h][a], g_rows[h], g_list, a)
 
         x_picked = [[keep.tile([P, PASS], F32, name="x_picked%d%d" % (h, a)) for a in range(PASSES)] for h in range(HALVES)]
         g_picked = [[keep.tile([P, PASS], F32, name="g_picked%d%d" % (h, a)) for a in range(PASSES)] for h in range(HALVES)]
@@ -81,7 +87,7 @@ def tile_list_moment_sized_bounded_shares_kernel(tc, xf, ca, gt, rb, cp, bn, off
 
         def x_turn(h, a):
             for t in range(PACK):
-                nc.tensor.transpose(x_ps[h][a][:, t, :], x_picked[h][a][:, t * P : (t + 1) * P], ident[:])
+                nc.tensor.transpose(x_ps[h][a][:, t, :], x_picked[h][a][:, t:PASS:PACK], ident[:])
 
         def x_size(h, a):
             for t in range(PACK):
@@ -98,7 +104,7 @@ def tile_list_moment_sized_bounded_shares_kernel(tc, xf, ca, gt, rb, cp, bn, off
         def u_factor(a):
             nc.vector.scalar_tensor_tensor(denom[a][:], mean_part[a][:, 1, :], 0.1, mean_part[a][:, 0, :], ALU.add, ALU.add)
             nc.vector.reciprocal(inverse[a][:], denom[a][:])
-            nc.vector.tensor_tensor(factor[a][:], inverse[a][:], ca_sb[:, a, :], ALU.mult)
+            nc.vector.tensor_tensor(factor[a][:], inverse[a][:], ca_sb[:, a, 0:PACK], ALU.mult)
 
         def u_scale(a, h):
             nc.vector.tensor_tensor(
@@ -111,14 +117,16 @@ def tile_list_moment_sized_bounded_shares_kernel(tc, xf, ca, gt, rb, cp, bn, off
         def u_quantise(a):
             nc.vector.quantize_mx(out=u_codes[a][:].bitcast(E4M3), scales=u_scales[a][:], in_=u_bf[a][:].rearrange("p k t -> p (k t)"))
 
-        g_bf = [[keep.tile([P, PASS], BF16, name="g_bf%d%d" % (h, a)) for a in range(PASSES)] for h in range(HALVES)]
+        g_bf = {}
         g_grouped = [[keep.tile([P, P * PACK], BF16, name="g_grouped%d%d" % (h, a), align_bytes=64) for a in range(PASSES)] for h in range(HALVES)]
         g_codes = [[keep.tile([P, P], U32, name="g_codes%d%d" % (h, a), align_bytes=64) for a in range(PASSES)] for h in range(HALVES)]
         g_scales = [[keep.tile([P, P], U8, name="g_scales%d%d" % (h, a), align_bytes=64) for a in range(PASSES)] for h in range(HALVES)]
 
         def g_weigh(h, a):
+            tag = "g_bf%d%d" % (h, a)
+            g_bf[h, a] = keep.tile([P, PASS], BF16, name="g_bf%d%d" % (h, a), tag=tag)
             nc.vector.scalar_tensor_tensor(
-                g_bf[h][a][:].rearrange("n (p t) -> n p t", t=PACK),
+                g_bf[h, a][:].rearrange("n (p t) -> n p t", t=PACK),
                 g_picked[h][a][:].rearrange("n (p t) -> n p t", t=PACK),
                 cp_sb[:, h : h + 1],
                 rb_ps[a][:].rearrange("n t p -> n p t"),
@@ -127,7 +135,7 @@ def tile_list_moment_sized_bounded_shares_kernel(tc, xf, ca, gt, rb, cp, bn, off
             )
 
         def g_turn(h, a):
-            words = g_bf[h][a][:].bitcast(F32)
+            words = g_bf[h, a][:].bitcast(F32)
             g_ps = psum.tile([P, 2, P], F32, name="g_ps%d%d" % (h, a), tag="g%d" % a)
             for u in range(2):
                 nc.tensor.transpose(g_ps[:, u, :], words[:, u : PASS // 2 : 2], ident[:])
@@ -140,59 +148,70 @@ def tile_list_moment_sized_bounded_shares_kernel(tc, xf, ca, gt, rb, cp, bn, off
         neg_logit = [keep.tile([P, HALVES, P], F32, name="neg_logit%d" % kh) for kh in range(HALVES)]
         neg_max = [keep.tile([P, HALVES], F32, name="neg_max%d" % kh) for kh in range(HALVES)]
 
-        def moment(h):
-            w_ps = psum.tile([P, HALVES, P], F32, name="w_ps%d" % h, tag="x%d0" % h)
-            for a in range(PASSES):
-                for kh in range(HALVES):
-                    nc.tensor.matmul_mx(
-                        out=w_ps[:, kh, :],
-                        lhsT=u_codes[a][:, kh * P : (kh + 1) * P].bitcast(E4M3),
-                        lhsT_scale=u_scales[a][:, kh * P : (kh + 1) * P],
-                        rhs=g_codes[h][a][:].bitcast(E5M2),
-                        rhs_scale=g_scales[h][a][:],
-                        start=(a == 0 and kh == 0),
-                        stop=(a == PASSES - 1 and kh == HALVES - 1),
-                    )
+        w_ps = {}
+
+        def product(h, a):
+            if a == 0:
+                w_ps[h] = psum.tile([P, HALVES, P], F32, name="w_ps%d" % h, tag="x%d0" % h)
             for kh in range(HALVES):
-                nc.vector.scalar_tensor_tensor(logit[:, h, kh, :], w_ps[:, kh, :], 0.02, bn_all[:, h, :], ALU.mult, ALU.add)
+                nc.tensor.matmul_mx(
+                    out=w_ps[h][:, kh, :],
+                    lhsT=u_codes[a][:, kh * P : (kh + 1) * P].bitcast(E4M3),
+                    lhsT_scale=u_scales[a][:, kh * P : (kh + 1) * P],
+                    rhs=g_codes[h][a][:].bitcast(E5M2),
+                    rhs_scale=g_scales[h][a][:],
+                    start=(a == 0 and kh == 0),
+                    stop=(a == PASSES - 1 and kh == HALVES - 1),
+                )
+
+        def logits(h):
+            for kh in range(HALVES):
+                nc.vector.scalar_tensor_tensor(logit[:, h, kh, :], w_ps[h][:, kh, :], 0.02, bn_all[:, h, :], ALU.mult, ALU.add)
             for kh in range(HALVES):
                 nc.vector.tensor_scalar(
                     neg_logit[kh][:, h, :], logit[:, h, kh, :], -1.0, neg_max[kh][:, 0:1] if h else None,
                     ALU.mult, ALU.min, accum_out=neg_max[kh][:, h : h + 1],
                 )
 
-        for h in range(HALVES):
-            for a in range(PASSES):
-                x_gather(h, a)
-                x_turn(h, a)
-                if (h, a) == (1, 1):
-                    g_gather(0, 0)
-                x_size(h, a)
-        g_gather(0, 1)
-        g_gather(1, 0)
-        g_gather(1, 1)
+        x_gather("vector", 0, 0)
+        x_gather("vector", 0, 1)
+        for a in range(PASSES):
+            x_turn(0, a)
+            x_size(0, a)
+        for a in range(PASSES):
+            x_gather("vector", 1, a)
+            x_turn(1, a)
+            if a == 1:
+                g_gather("scalar", 0, 0)
+            x_size(1, a)
+        g_gather("scalar", 0, 1)
+        g_gather("scalar", 1, 0)
+        g_gather("scalar", 1, 1)
         u_factor(0)
-        u_scale(0, 0)
-        u_scale(0, 1)
         u_factor(1)
-        u_quantise(0)
-        u_scale(1, 0)
-        u_scale(1, 1)
+        for a in range(PASSES):
+            for h in range(HALVES):
+                u_scale(a, h)
         g_weigh(0, 0)
-        u_quantise(1)
         g_weigh(0, 1)
+        u_quantise(0)
         g_weigh(1, 0)
+        u_quantise(1)
+        g_weigh(1, 1)
         g_turn(0, 0)
         g_turn(0, 1)
         g_turn(1, 0)
-        g_weigh(1, 1)
         g_quantise(0, 0)
         g_quantise(0, 1)
+        product(0, 0)
+        product(0, 1)
         g_turn(1, 1)
-        moment(0)
         g_quantise(1, 0)
+        product(1, 0)
         g_quantise(1, 1)
-        moment(1)
+        product(1, 1)
+        logits(0)
+        logits(1)
 
         for kh in range(HALVES):
             shares = keep.tile([P, P, HALVES], F32, name="shares%d" % kh)

@@ -40,7 +40,6 @@ def tile_list_moment_sized_bounded_shares_kernel(tc, xf, ca, gt, rb, cp, bn, off
         bn_sb = keep.tile([P, HALVES], F32, name="bn_sb")
         g_by_parity = gt.rearrange("(p h) v -> h p v", h=HALVES)
 
-        nc.scalar.dma_start(bn_sb[:], bn.rearrange("o (p h) -> p (o h)", h=HALVES))
         nc.scalar.dma_start(rb_sb[:, :, 0:PACK], rb.rearrange("o (a p t) -> p (o a) t", p=P, t=PACK))
         nc.sync.dma_start(x_list[:], offs)
         nc.sync.dma_start(x_rows[0][:], xf[0:P, :])
@@ -48,17 +47,13 @@ def tile_list_moment_sized_bounded_shares_kernel(tc, xf, ca, gt, rb, cp, bn, off
         nc.sync.dma_start(ca_sb[:, :, 0:PACK], ca.rearrange("(a p t) o -> p a (t o)", p=P, t=PACK))
         nc.sync.dma_start(g_list[:], offs2)
         nc.sync.dma_start(g_rows[0][:], g_by_parity[0])
+        nc.sync.dma_start(bn_sb[:], bn.rearrange("o (p h) -> p (o h)", h=HALVES))
         nc.sync.dma_start(cp_sb[:], cp.rearrange("(p h) o -> p (h o)", h=HALVES))
         nc.sync.dma_start(g_rows[1][:], g_by_parity[1])
 
         ident = keep.tile([P, P], F32, name="ident")
         make_identity(nc, ident[:])
 
-        bn_ps = psum.tile([P, HALVES, P], F32, name="bn_ps", tag="g0")
-        for h in range(HALVES):
-            nc.tensor.transpose(bn_ps[:, h, :], bn_sb[:, h : h + 1].to_broadcast([P, P]), ident[:])
-        bn_all = keep.tile([P, HALVES, P], F32, name="bn_all")
-        nc.scalar.activation(bn_all[:], bn_ps[:], ACT.Copy)
         rb_ps = [psum.tile([P, PACK, P], F32, name="rb_ps%d" % a, tag="rb%d" % a) for a in range(PASSES)]
         for a in range(PASSES):
             for t in range(PACK):
@@ -97,13 +92,13 @@ def tile_list_moment_sized_bounded_shares_kernel(tc, xf, ca, gt, rb, cp, bn, off
         u_codes = [keep.tile([P, K], U32, name="u_codes%d" % a, align_bytes=64) for a in range(PASSES)]
         u_scales = [keep.tile([P, K], U8, name="u_scales%d" % a, align_bytes=64) for a in range(PASSES)]
         u_bf = [keep.tile([P, K, PACK], BF16, name="u_bf%d" % a, align_bytes=64) for a in range(PASSES)]
-        denom = [keep.tile([P, PACK], F32, name="denom%d" % a) for a in range(PASSES)]
         inverse = [keep.tile([P, PACK], F32, name="inverse%d" % a) for a in range(PASSES)]
         factor = [keep.tile([P, PACK], F32, name="factor%d" % a) for a in range(PASSES)]
 
         def u_factor(a):
-            nc.vector.scalar_tensor_tensor(denom[a][:], mean_part[a][:, 1, :], 0.1, mean_part[a][:, 0, :], ALU.add, ALU.add)
-            nc.vector.reciprocal(inverse[a][:], denom[a][:])
+            denom = keep.tile([P, PACK], F32, name="denom%d" % a, tag="bn_sb" if a == 0 else "denom1")
+            nc.vector.scalar_tensor_tensor(denom[:], mean_part[a][:, 1, :], 0.1, mean_part[a][:, 0, :], ALU.add, ALU.add)
+            nc.vector.reciprocal(inverse[a][:], denom[:])
             nc.vector.tensor_tensor(factor[a][:], inverse[a][:], ca_sb[:, a, 0:PACK], ALU.mult)
 
         def u_scale(a, h):
@@ -118,12 +113,12 @@ def tile_list_moment_sized_bounded_shares_kernel(tc, xf, ca, gt, rb, cp, bn, off
             nc.vector.quantize_mx(out=u_codes[a][:].bitcast(E4M3), scales=u_scales[a][:], in_=u_bf[a][:].rearrange("p k t -> p (k t)"))
 
         g_bf = {}
-        g_grouped = [[keep.tile([P, P * PACK], BF16, name="g_grouped%d%d" % (h, a), align_bytes=64) for a in range(PASSES)] for h in range(HALVES)]
-        g_codes = [[keep.tile([P, P], U32, name="g_codes%d%d" % (h, a), align_bytes=64) for a in range(PASSES)] for h in range(HALVES)]
-        g_scales = [[keep.tile([P, P], U8, name="g_scales%d%d" % (h, a), align_bytes=64) for a in range(PASSES)] for h in range(HALVES)]
+        g_grouped = [keep.tile([P, HALVES, P * PACK], BF16, name="g_grouped%d" % a, align_bytes=64) for a in range(PASSES)]
+        g_codes = [keep.tile([P, N], U32, name="g_codes%d" % a, align_bytes=64) for a in range(PASSES)]
+        g_scales = [keep.tile([P, N], U8, name="g_scales%d" % a, align_bytes=64) for a in range(PASSES)]
 
         def g_weigh(h, a):
-            tag = "g_bf%d%d" % (h, a)
+            tag = {(0, 0): "mean_part0", (0, 1): "factor0", (1, 0): "g_picked01", (1, 1): "g_picked10"}[h, a]
             g_bf[h, a] = keep.tile([P, PASS], BF16, name="g_bf%d%d" % (h, a), tag=tag)
             nc.vector.scalar_tensor_tensor(
                 g_bf[h, a][:].rearrange("n (p t) -> n p t", t=PACK),
@@ -139,38 +134,25 @@ def tile_list_moment_sized_bounded_shares_kernel(tc, xf, ca, gt, rb, cp, bn, off
             g_ps = psum.tile([P, 2, P], F32, name="g_ps%d%d" % (h, a), tag="g%d" % a)
             for u in range(2):
                 nc.tensor.transpose(g_ps[:, u, :], words[:, u : PASS // 2 : 2], ident[:])
-            nc.scalar.copy(g_grouped[h][a][:].bitcast(F32).rearrange("p (n u) -> p n u", u=2), g_ps[:].rearrange("p u n -> p n u"))
+            nc.scalar.copy(g_grouped[a][:, h, :].bitcast(F32).rearrange("p (n u) -> p n u", u=2), g_ps[:].rearrange("p u n -> p n u"))
 
-        def g_quantise(h, a):
-            nc.vector.quantize_mx(out=g_codes[h][a][:].bitcast(E5M2), scales=g_scales[h][a][:], in_=g_grouped[h][a][:])
-
-        logit = keep.tile([P, HALVES, HALVES, P], F32, name="logit")
-        neg_logit = [keep.tile([P, HALVES, P], F32, name="neg_logit%d" % kh) for kh in range(HALVES)]
-        neg_max = [keep.tile([P, HALVES], F32, name="neg_max%d" % kh) for kh in range(HALVES)]
+        def g_quantise(a):
+            nc.vector.quantize_mx(out=g_codes[a][:].bitcast(E5M2), scales=g_scales[a][:], in_=g_grouped[a][:].rearrange("p h c -> p (h c)"))
 
         w_ps = {}
 
-        def product(h, a):
-            if a == 0:
-                w_ps[h] = psum.tile([P, HALVES, P], F32, name="w_ps%d" % h, tag="x%d0" % h)
+        def product(a):
             for kh in range(HALVES):
+                if a == 0:
+                    w_ps[kh] = psum.tile([P, N], F32, name="w_ps%d" % kh, tag="x%d0" % kh)
                 nc.tensor.matmul_mx(
-                    out=w_ps[h][:, kh, :],
+                    out=w_ps[kh][:],
                     lhsT=u_codes[a][:, kh * P : (kh + 1) * P].bitcast(E4M3),
                     lhsT_scale=u_scales[a][:, kh * P : (kh + 1) * P],
-                    rhs=g_codes[h][a][:].bitcast(E5M2),
-                    rhs_scale=g_scales[h][a][:],
-                    start=(a == 0 and kh == 0),
-                    stop=(a == PASSES - 1 and kh == HALVES - 1),
-                )
-
-        def logits(h):
-            for kh in range(HALVES):
-                nc.vector.scalar_tensor_tensor(logit[:, h, kh, :], w_ps[h][:, kh, :], 0.02, bn_all[:, h, :], ALU.mult, ALU.add)
-            for kh in range(HALVES):
-                nc.vector.tensor_scalar(
-                    neg_logit[kh][:, h, :], logit[:, h, kh, :], -1.0, neg_max[kh][:, 0:1] if h else None,
-                    ALU.mult, ALU.min, accum_out=neg_max[kh][:, h : h + 1],
+                    rhs=g_codes[a][:].bitcast(E5M2),
+                    rhs_scale=g_scales[a][:],
+                    start=(a == 0),
+                    stop=(a == PASSES - 1),
                 )
 
         x_gather("vector", 0, 0)
@@ -181,38 +163,41 @@ def tile_list_moment_sized_bounded_shares_kernel(tc, xf, ca, gt, rb, cp, bn, off
         for a in range(PASSES):
             x_gather("vector", 1, a)
             x_turn(1, a)
-            if a == 1:
-                g_gather("scalar", 0, 0)
             x_size(1, a)
+        g_gather("vector", 0, 0)
         g_gather("scalar", 0, 1)
         g_gather("scalar", 1, 0)
         g_gather("scalar", 1, 1)
+        bn_ps = psum.tile([P, HALVES, P], F32, name="bn_ps", tag="g1")
+        for h in range(HALVES):
+            nc.tensor.transpose(bn_ps[:, h, :], bn_sb[:, h : h + 1].to_broadcast([P, P]), ident[:])
+        bn_all = keep.tile([P, HALVES, P], F32, name="bn_all")
+        nc.scalar.activation(bn_all[:], bn_ps[:], ACT.Copy)
         u_factor(0)
         u_factor(1)
-        for a in range(PASSES):
-            for h in range(HALVES):
-                u_scale(a, h)
         g_weigh(0, 0)
+        u_scale(0, 0)
+        u_scale(0, 1)
         g_weigh(0, 1)
-        u_quantise(0)
         g_weigh(1, 0)
-        u_quantise(1)
+        u_scale(1, 0)
         g_weigh(1, 1)
-        g_turn(0, 0)
-        g_turn(0, 1)
-        g_turn(1, 0)
-        g_quantise(0, 0)
-        g_quantise(0, 1)
-        product(0, 0)
-        product(0, 1)
-        g_turn(1, 1)
-        g_quantise(1, 0)
-        product(1, 0)
-        g_quantise(1, 1)
-        product(1, 1)
-        logits(0)
-        logits(1)
+        u_scale(1, 1)
+        for h in range(HALVES):
+            for a in range(PASSES):
+                g_turn(h, a)
+        for a in range(PASSES):
+            u_quantise(a)
+            g_quantise(a)
+            product(a)
 
+        logit = [keep.tile([P, N], F32, name="logit%d" % kh) for kh in range(HALVES)]
+        neg_logit = [keep.tile([P, HALVES, P], F32, name="neg_logit%d" % kh) for kh in range(HALVES)]
+        neg_max = [keep.tile([P, 1], F32, name="neg_max%d" % kh) for kh in range(HALVES)]
+        for kh in range(HALVES):
+            nc.vector.scalar_tensor_tensor(logit[kh][:], w_ps[kh][:], 0.02, bn_all[:].rearrange("k h p -> k (h p)"), ALU.mult, ALU.add)
+        for kh in range(HALVES):
+            nc.vector.tensor_scalar(neg_logit[kh][:].rearrange("k h p -> k (h p)"), logit[kh][:], -1.0, None, ALU.mult, ALU.min, accum_out=neg_max[kh][:])
         for kh in range(HALVES):
             shares = keep.tile([P, P, HALVES], F32, name="shares%d" % kh)
             total = keep.tile([P, 1], F32, name="total%d" % kh)
@@ -220,7 +205,7 @@ def tile_list_moment_sized_bounded_shares_kernel(tc, xf, ca, gt, rb, cp, bn, off
             result = keep.tile([P, N], F32, name="result%d" % kh)
             nc.scalar.activation(
                 shares[:], neg_logit[kh][:].rearrange("k h p -> k p h"), ACT.Exp,
-                bias=neg_max[kh][:, 1:2], scale=-1.0, accum_out=total[:],
+                bias=neg_max[kh][:], scale=-1.0, accum_out=total[:],
             )
             nc.vector.reciprocal(inv_total[:], total[:])
             nc.vector.tensor_scalar(result[:], shares[:].rearrange("k p h -> k (p h)"), inv_total[:], 256.0, ALU.mult, ALU.mult)

@@ -22,6 +22,7 @@ PASS = P * PACK
 PASSES = J // PASS
 HALVES = 2
 PER_COLUMN = 16
+PAIRS = PACK // 2
 
 
 def tile_list_moment_sized_bounded_shares_kernel(tc, xf, ca, gt, rb, cp, bn, offs, offs2, out):
@@ -40,14 +41,14 @@ def tile_list_moment_sized_bounded_shares_kernel(tc, xf, ca, gt, rb, cp, bn, off
         bn_sb = keep.tile([P, HALVES], F32, name="bn_sb")
         g_by_parity = gt.rearrange("(p h) v -> h p v", h=HALVES)
 
-        nc.scalar.dma_start(rb_sb[:, :, 0:PACK], rb.rearrange("o (a p t) -> p (o a) t", p=P, t=PACK))
         nc.sync.dma_start(x_list[:], offs)
         nc.sync.dma_start(x_rows[0][:], xf[0:P, :])
+        nc.sync.dma_start(rb_sb[:, :, 0:PACK], rb.rearrange("o (a p t) -> p (o a) t", p=P, t=PACK))
         nc.sync.dma_start(x_rows[1][:], xf[P : 2 * P, :])
-        nc.sync.dma_start(ca_sb[:, :, 0:PACK], ca.rearrange("(a p t) o -> p a (t o)", p=P, t=PACK))
         nc.sync.dma_start(g_list[:], offs2)
         nc.sync.dma_start(g_rows[0][:], g_by_parity[0])
         nc.sync.dma_start(bn_sb[:], bn.rearrange("o (p h) -> p (o h)", h=HALVES))
+        nc.sync.dma_start(ca_sb[:, :, 0:PACK], ca.rearrange("(a p t) o -> p a (t o)", p=P, t=PACK))
         nc.sync.dma_start(cp_sb[:], cp.rearrange("(p h) o -> p (h o)", h=HALVES))
         nc.sync.dma_start(g_rows[1][:], g_by_parity[1])
 
@@ -59,26 +60,17 @@ def tile_list_moment_sized_bounded_shares_kernel(tc, xf, ca, gt, rb, cp, bn, off
             for t in range(PACK):
                 nc.tensor.transpose(rb_ps[a][:, t, :], rb_sb[:, a, t : t + 1].to_broadcast([P, P]), ident[:])
 
-        def slots(offsets, a):
-            return offsets[:, a * PASS // PER_COLUMN : (a + 1) * PASS // PER_COLUMN]
-
-        def gather(engine, picked, rows, offsets, a):
-            if engine == "vector":
-                nc.vector.tensor_copy(picked[:], rows[:].indirect(slots(offsets, a)))
-            else:
-                nc.scalar.activation(picked[:], rows[:].indirect(slots(offsets, a)), ACT.Copy)
-
-        def x_gather(engine, h, a):
-            gather(engine, x_picked[h][a], x_rows[h], x_list, a)
-
-        def g_gather(engine, h, a):
-            gather(engine, g_picked[h][a], g_rows[h], g_list, a)
-
         x_picked = [[keep.tile([P, PASS], F32, name="x_picked%d%d" % (h, a)) for a in range(PASSES)] for h in range(HALVES)]
         g_picked = [[keep.tile([P, PASS], F32, name="g_picked%d%d" % (h, a)) for a in range(PASSES)] for h in range(HALVES)]
         x_ps = [[psum.tile([P, PACK, P], F32, name="x_ps%d%d" % (h, a), tag="x%d%d" % (h, a)) for a in range(PASSES)] for h in range(HALVES)]
         mean_part = [keep.tile([P, HALVES, PACK], F32, name="mean_part%d" % a) for a in range(PASSES)]
         magnitude = keep.tile([P, HALVES, PASSES, PACK, P], BF16, name="magnitude")
+
+        def listed(rows, offsets, a):
+            return rows[:].indirect(offsets[:, a * PASS // PER_COLUMN : (a + 1) * PASS // PER_COLUMN])
+
+        def x_gather(h, a):
+            nc.vector.tensor_copy(x_picked[h][a][:], listed(x_rows[h], x_list, a))
 
         def x_turn(h, a):
             for t in range(PACK):
@@ -87,7 +79,6 @@ def tile_list_moment_sized_bounded_shares_kernel(tc, xf, ca, gt, rb, cp, bn, off
         def x_size(h, a):
             for t in range(PACK):
                 nc.scalar.activation(magnitude[:, h, a, t, :], x_ps[h][a][:, t, :], ACT.Abs, scale=1.0 / K, accum_out=mean_part[a][:, h, t : t + 1])
-
 
         u_codes = [keep.tile([P, K], U32, name="u_codes%d" % a, align_bytes=64) for a in range(PASSES)]
         u_scales = [keep.tile([P, K], U8, name="u_scales%d" % a, align_bytes=64) for a in range(PASSES)]
@@ -117,9 +108,10 @@ def tile_list_moment_sized_bounded_shares_kernel(tc, xf, ca, gt, rb, cp, bn, off
         g_codes = [keep.tile([P, N], U32, name="g_codes%d" % a, align_bytes=64) for a in range(PASSES)]
         g_scales = [keep.tile([P, N], U8, name="g_scales%d" % a, align_bytes=64) for a in range(PASSES)]
 
+        weigh_after = {(0, 0): "mean_part0", (0, 1): "factor0", (1, 0): "g_picked01", (1, 1): "g_picked10"}
+
         def g_weigh(h, a):
-            tag = {(0, 0): "mean_part0", (0, 1): "factor0", (1, 0): "g_picked01", (1, 1): "g_picked10"}[h, a]
-            g_bf[h, a] = keep.tile([P, PASS], BF16, name="g_bf%d%d" % (h, a), tag=tag)
+            g_bf[h, a] = keep.tile([P, PASS], BF16, name="g_bf%d%d" % (h, a), tag=weigh_after[h, a])
             nc.vector.scalar_tensor_tensor(
                 g_bf[h, a][:].rearrange("n (p t) -> n p t", t=PACK),
                 g_picked[h][a][:].rearrange("n (p t) -> n p t", t=PACK),
@@ -129,12 +121,14 @@ def tile_list_moment_sized_bounded_shares_kernel(tc, xf, ca, gt, rb, cp, bn, off
                 ALU.mult,
             )
 
+        turn_bank = {(0, 0): "g0", (0, 1): "x01", (1, 0): "g0", (1, 1): "g1"}
+
         def g_turn(h, a):
             words = g_bf[h, a][:].bitcast(F32)
-            g_ps = psum.tile([P, 2, P], F32, name="g_ps%d%d" % (h, a), tag="g%d" % a)
-            for u in range(2):
-                nc.tensor.transpose(g_ps[:, u, :], words[:, u : PASS // 2 : 2], ident[:])
-            nc.scalar.copy(g_grouped[a][:, h, :].bitcast(F32).rearrange("p (n u) -> p n u", u=2), g_ps[:].rearrange("p u n -> p n u"))
+            g_ps = psum.tile([P, PAIRS, P], F32, name="g_ps%d%d" % (h, a), tag=turn_bank[h, a])
+            for u in range(PAIRS):
+                nc.tensor.transpose(g_ps[:, u, :], words[:, u : P * PAIRS : PAIRS], ident[:])
+            nc.scalar.copy(g_grouped[a][:, h, :].bitcast(F32).rearrange("p (n u) -> p n u", u=PAIRS), g_ps[:].rearrange("p u n -> p n u"))
 
         def g_quantise(a):
             nc.vector.quantize_mx(out=g_codes[a][:].bitcast(E5M2), scales=g_scales[a][:], in_=g_grouped[a][:].rearrange("p h c -> p (h c)"))
@@ -155,24 +149,25 @@ def tile_list_moment_sized_bounded_shares_kernel(tc, xf, ca, gt, rb, cp, bn, off
                     stop=(a == PASSES - 1),
                 )
 
-        x_gather("vector", 0, 0)
-        x_gather("vector", 0, 1)
+        for a in range(PASSES):
+            x_gather(0, a)
         for a in range(PASSES):
             x_turn(0, a)
             x_size(0, a)
         for a in range(PASSES):
-            x_gather("vector", 1, a)
+            x_gather(1, a)
             x_turn(1, a)
             x_size(1, a)
-        g_gather("vector", 0, 0)
-        g_gather("scalar", 0, 1)
-        g_gather("scalar", 1, 0)
-        g_gather("scalar", 1, 1)
+        nc.vector.tensor_copy(g_picked[0][0][:], listed(g_rows[0], g_list, 0))
+        for h, a in ((0, 1), (1, 0), (1, 1)):
+            nc.scalar.activation(g_picked[h][a][:], listed(g_rows[h], g_list, a), ACT.Copy)
+
         bn_ps = psum.tile([P, HALVES, P], F32, name="bn_ps", tag="g1")
         for h in range(HALVES):
             nc.tensor.transpose(bn_ps[:, h, :], bn_sb[:, h : h + 1].to_broadcast([P, P]), ident[:])
         bn_all = keep.tile([P, HALVES, P], F32, name="bn_all")
         nc.scalar.activation(bn_all[:], bn_ps[:], ACT.Copy)
+
         u_factor(0)
         u_factor(1)
         g_weigh(0, 0)

from contextlib import ExitStack

import concourse.mybir as mybir
from concourse.masks import make_identity

K, J, N, T = 256, 1024, 256, 2048
FLOPS = 2 * K * J * N

F32 = mybir.dt.float32
BF16 = mybir.dt.bfloat16
U32 = mybir.dt.uint32
U16 = mybir.dt.uint16
U8 = mybir.dt.uint8
E4M3 = mybir.dt.float8_e4m3fn_x4
E5M2 = mybir.dt.float8_e5m2_x4
ALU = mybir.AluOpType
ACT = mybir.ActivationFunctionType

P = 128
PACK = 4
PASS = P * PACK
PASSES = J // PASS
HALVES = 2
PER_COLUMN = 16
PAIRS = PACK // 2


def tile_list_moment_sized_bounded_shares_kernel(tc, xf, ca, gt, rb, cp, bn, offs, offs2, out):
    nc = tc.nc
    with ExitStack() as ctx:
        keep = ctx.enter_context(tc.tile_pool(name="keep", bufs=1))
        psum = ctx.enter_context(tc.psum_pool(name="psum", bufs=1))

        x_list = keep.tile([P, J // PER_COLUMN], U16, name="x_list")
        g_list = keep.tile([P, J // PER_COLUMN], U16, name="g_list")
        x_rows = [keep.tile([P, T], F32, name="x_rows%d" % h) for h in range(HALVES)]
        g_rows = [keep.tile([P, T], F32, name="g_rows%d" % h) for h in range(HALVES)]
        ca_sb = keep.tile([P, PASSES, 2 * PACK], F32, name="ca_sb")
        rb_sb = keep.tile([P, PASSES, 2 * PACK], F32, name="rb_sb")
        cp_sb = keep.tile([P, HALVES], F32, name="cp_sb")
        bn_sb = keep.tile([P, HALVES], F32, name="bn_sb")
        g_by_parity = gt.rearrange("(p h) v -> h p v", h=HALVES)

        nc.sync.dma_start(x_list[:], offs)
        nc.sync.dma_start(x_rows[0][:], xf[0:P, :])
        nc.sync.dma_start(rb_sb[:, :, 0:PACK], rb.rearrange("o (a p t) -> p (o a) t", p=P, t=PACK))
        nc.sync.dma_start(x_rows[1][:], xf[P : 2 * P, :])
        nc.sync.dma_start(g_list[:], offs2)
        nc.sync.dma_start(g_rows[0][:], g_by_parity[0])
        nc.sync.dma_start(bn_sb[:], bn.rearrange("o (p h) -> p (o h)", h=HALVES))
        nc.sync.dma_start(ca_sb[:, :, 0:PACK], ca.rearrange("(a p t) o -> p a (t o)", p=P, t=PACK))
        nc.sync.dma_start(cp_sb[:], cp.rearrange("(p h) o -> p (h o)", h=HALVES))
        nc.sync.dma_start(g_rows[1][:], g_by_parity[1])

        ident = keep.tile([P, P], F32, name="ident")
        make_identity(nc, ident[:])

        rb_ps = [psum.tile([P, PACK, P], F32, name="rb_ps%d" % a, tag="rb%d" % a) for a in range(PASSES)]
        for a in range(PASSES):
            for t in range(PACK):
                nc.tensor.transpose(rb_ps[a][:, t, :], rb_sb[:, a, t : t + 1].to_broadcast([P, P]), ident[:])

        x_picked = [[keep.tile([P, PASS], F32, name="x_picked%d%d" % (h, a)) for a in range(PASSES)] for h in range(HALVES)]
        g_picked = [[keep.tile([P, PASS], F32, name="g_picked%d%d" % (h, a)) for a in range(PASSES)] for h in range(HALVES)]
        x_ps = [[psum.tile([P, PACK, P], F32, name="x_ps%d%d" % (h, a), tag="x%d%d" % (h, a)) for a in range(PASSES)] for h in range(HALVES)]
        mean_part = [keep.tile([P, HALVES, PACK], F32, name="mean_part%d" % a) for a in range(PASSES)]
        magnitude = keep.tile([P, HALVES, PASSES, PACK, P], BF16, name="magnitude")

        def listed(rows, offsets, a):
            return rows[:].indirect(offsets[:, a * PASS // PER_COLUMN : (a + 1) * PASS // PER_COLUMN])

        def x_gather(h, a):
            nc.vector.tensor_copy(x_picked[h][a][:], listed(x_rows[h], x_list, a))

        def x_turn(h, a):
            for t in range(PACK):
                nc.tensor.transpose(x_ps[h][a][:, t, :], x_picked[h][a][:, t:PASS:PACK], ident[:])

        def x_size(h, a):
            for t in range(PACK):
                nc.scalar.activation(magnitude[:, h, a, t, :], x_ps[h][a][:, t, :], ACT.Abs, scale=1.0 / K, accum_out=mean_part[a][:, h, t : t + 1])

        u_codes = [keep.tile([P, K], U32, name="u_codes%d" % a, align_bytes=64) for a in range(PASSES)]
        u_scales = [keep.tile([P, K], U8, name="u_scales%d" % a, align_bytes=64) for a in range(PASSES)]
        u_bf = [keep.tile([P, K, PACK], BF16, name="u_bf%d" % a, align_bytes=64) for a in range(PASSES)]
        inverse = [keep.tile([P, PACK], F32, name="inverse%d" % a) for a in range(PASSES)]
        factor = [keep.tile([P, PACK], F32, name="factor%d" % a) for a in range(PASSES)]

        def u_factor(a):
            denom = keep.tile([P, PACK], F32, name="denom%d" % a, tag="bn_sb" if a == 0 else "denom1")
            nc.vector.scalar_tensor_tensor(denom[:], mean_part[a][:, 1, :], 0.1, mean_part[a][:, 0, :], ALU.add, ALU.add)
            nc.vector.reciprocal(inverse[a][:], denom[:])
            nc.vector.tensor_tensor(factor[a][:], inverse[a][:], ca_sb[:, a, 0:PACK], ALU.mult)

        def u_scale(a, h):
            nc.vector.tensor_tensor(
                u_bf[a][:, h * P : (h + 1) * P, :],
                x_ps[h][a][:].rearrange("p t k -> p k t"),
                factor[a][:].unsqueeze(1).to_broadcast([P, P, PACK]),
                ALU.mult,
            )

        def u_quantise(a):
            nc.vector.quantize_mx(out=u_codes[a][:].bitcast(E4M3), scales=u_scales[a][:], in_=u_bf[a][:].rearrange("p k t -> p (k t)"))

        g_bf = {}
        g_grouped = [keep.tile([P, HALVES, P * PACK], BF16, name="g_grouped%d" % a, align_bytes=64) for a in range(PASSES)]
        g_codes = [keep.tile([P, N], U32, name="g_codes%d" % a, align_bytes=64) for a in range(PASSES)]
        g_scales = [keep.tile([P, N], U8, name="g_scales%d" % a, align_bytes=64) for a in range(PASSES)]

        weigh_after = {(0, 0): "mean_part0", (0, 1): "factor0", (1, 0): "g_picked01", (1, 1): "g_picked10"}

        def g_weigh(h, a):
            g_bf[h, a] = keep.tile([P, PASS], BF16, name="g_bf%d%d" % (h, a), tag=weigh_after[h, a])
            nc.vector.scalar_tensor_tensor(
                g_bf[h, a][:].rearrange("n (p t) -> n p t", t=PACK),
                g_picked[h][a][:].rearrange("n (p t) -> n p t", t=PACK),
                cp_sb[:, h : h + 1],
                rb_ps[a][:].rearrange("n t p -> n p t"),
                ALU.min,
                ALU.mult,
            )

        turn_bank = {(0, 0): "g0", (0, 1): "x01", (1, 0): "g0", (1, 1): "g1"}

        def g_turn(h, a):
            words = g_bf[h, a][:].bitcast(F32)
            g_ps = psum.tile([P, PAIRS, P], F32, name="g_ps%d%d" % (h, a), tag=turn_bank[h, a])
            for u in range(PAIRS):
                nc.tensor.transpose(g_ps[:, u, :], words[:, u : P * PAIRS : PAIRS], ident[:])
            nc.scalar.copy(g_grouped[a][:, h, :].bitcast(F32).rearrange("p (n u) -> p n u", u=PAIRS), g_ps[:].rearrange("p u n -> p n u"))

        def g_quantise(a):
            nc.vector.quantize_mx(out=g_codes[a][:].bitcast(E5M2), scales=g_scales[a][:], in_=g_grouped[a][:].rearrange("p h c -> p (h c)"))

        w_ps = {}

        def product(a):
            for kh in range(HALVES):
                if a == 0:
                    w_ps[kh] = psum.tile([P, N], F32, name="w_ps%d" % kh, tag="x%d0" % kh)
                nc.tensor.matmul_mx(
                    out=w_ps[kh][:],
                    lhsT=u_codes[a][:, kh * P : (kh + 1) * P].bitcast(E4M3),
                    lhsT_scale=u_scales[a][:, kh * P : (kh + 1) * P],
                    rhs=g_codes[a][:].bitcast(E5M2),
                    rhs_scale=g_scales[a][:],
                    start=(a == 0),
                    stop=(a == PASSES - 1),
                )

        for a in range(PASSES):
            x_gather(0, a)
        for a in range(PASSES):
            x_turn(0, a)
            x_size(0, a)
        for a in range(PASSES):
            x_gather(1, a)
            x_turn(1, a)
            x_size(1, a)
        nc.vector.tensor_copy(g_picked[0][0][:], listed(g_rows[0], g_list, 0))
        for h, a in ((0, 1), (1, 0), (1, 1)):
            nc.scalar.activation(g_picked[h][a][:], listed(g_rows[h], g_list, a), ACT.Copy)

        bn_ps = psum.tile([P, HALVES, P], F32, name="bn_ps", tag="g1")
        for h in range(HALVES):
            nc.tensor.transpose(bn_ps[:, h, :], bn_sb[:, h : h + 1].to_broadcast([P, P]), ident[:])
        bn_all = keep.tile([P, HALVES, P], F32, name="bn_all")
        nc.scalar.activation(bn_all[:], bn_ps[:], ACT.Copy)

        u_factor(0)
        u_factor(1)
        g_weigh(0, 0)
        u_scale(0, 0)
        u_scale(0, 1)
        g_weigh(0, 1)
        g_weigh(1, 0)
        u_scale(1, 0)
        g_weigh(1, 1)
        u_scale(1, 1)
        for h in range(HALVES):
            for a in range(PASSES):
                g_turn(h, a)
        for a in range(PASSES):
            u_quantise(a)
            g_quantise(a)
            product(a)

        logit = [keep.tile([P, N], F32, name="logit%d" % kh) for kh in range(HALVES)]
        neg_logit = [keep.tile([P, HALVES, P], F32, name="neg_logit%d" % kh) for kh in range(HALVES)]
        neg_max = [keep.tile([P, 1], F32, name="neg_max%d" % kh) for kh in range(HALVES)]
        for kh in range(HALVES):
            nc.vector.scalar_tensor_tensor(logit[kh][:], w_ps[kh][:], 0.02, bn_all[:].rearrange("k h p -> k (h p)"), ALU.mult, ALU.add)
        for kh in range(HALVES):
            nc.vector.tensor_scalar(neg_logit[kh][:].rearrange("k h p -> k (h p)"), logit[kh][:], -1.0, None, ALU.mult, ALU.min, accum_out=neg_max[kh][:])
        for kh in range(HALVES):
            shares = keep.tile([P, P, HALVES], F32, name="shares%d" % kh)
            total = keep.tile([P, 1], F32, name="total%d" % kh)
            inv_total = keep.tile([P, 1], F32, name="inv_total%d" % kh)
            result = keep.tile([P, N], F32, name="result%d" % kh)
            nc.scalar.activation(
                shares[:], neg_logit[kh][:].rearrange("k h p -> k p h"), ACT.Exp,
                bias=neg_max[kh][:], scale=-1.0, accum_out=total[:],
            )
            nc.vector.reciprocal(inv_total[:], total[:])
            nc.vector.tensor_scalar(result[:], shares[:].rearrange("k p h -> k (p h)"), inv_total[:], 256.0, ALU.mult, ALU.mult)
            nc.sync.dma_start(out[kh * P : (kh + 1) * P, :], result[:])
